import numpy as np, ml_dtypes
CORES = [10,34,74,98]
N = 4
import mx_ref
BF = ml_dtypes.bfloat16
def entries(a):
    return np.ascontiguousarray(a.T).reshape(-1)
def table(e):
    return np.ascontiguousarray(np.reshape(e, (-1, 16)).T).astype(np.int32)
def cut(t, i, w=512):
    return t[:, w * i:w * i + w]
def f(rng, *shape):
    return mx_ref.flush((rng.standard_normal(shape, dtype=np.float32) * np.exp2(rng.integers(-2, 3, shape[:-1] + (1,)))).astype(BF))
def wide(rng, *shape, cols=0):
    v = rng.standard_normal(shape, dtype=np.float32) * np.exp2(rng.integers(-12, 13, shape)).astype(np.float32)
    if cols: v *= np.repeat(np.exp2(rng.integers(-cols, cols + 1, shape[:-2] + (1, shape[-1] // 4))) * (rng.random(shape[:-2] + (1, shape[-1] // 4)) > 0.0625), 4, axis=-1).astype(np.float32)
    return mx_ref.flush(v.astype(BF))
E, NB = 4, 8
T, L, G = 128 * NB, 4 * NB, N * E
def listed(es):
    return {"ids": np.stack([table(e) for e in es])}
def setup_inputs(rng):
    return {"x": f(rng, N, 128, 4 * T), "wt": f(rng, N, 128, 512 * E), **listed([rng.integers(0, G, L) for r in range(N)])}
def setup_inputs_one(rng):
    return {**setup_inputs(rng), **listed([np.full(L, rng.integers(0, G))] * N)}
def setup_inputs_own(rng):
    return {**setup_inputs(rng), **listed([r * E + rng.integers(0, E, L) for r in range(N)])}
def setup_inputs_ends(rng):
    es = []
    for r in range(N):
        e = rng.choice([0, G - 1], L); e[rng.permutation(L)[:2]] = [0, G - 1]
        es.append(e)
    return {**setup_inputs(rng), **listed(es)}
def setup_inputs_each(rng):
    return {**setup_inputs(rng), **listed([np.concatenate([rng.permutation(G) for i in range(L // G + 1)])[:L] for r in range(N)])}
def setup_inputs_spread(rng):
    d = setup_inputs(rng); d["x"] = wide(rng, N, 128, 4 * T, cols=8); d["wt"] = wide(rng, N, 128, 512 * E, cols=8); return d
def check_inputs(d):
    b = []
    for r in range(N):
        e = entries(d["ids"][r])
        if e.min() < 0 or e.max() >= G: b.append("ids")
    return b
def reference(x, wt, ids):
    U = [mx_ref.quantize(np.ascontiguousarray(cut(wt[q], m))) for q in range(N) for m in range(E)]
    y = np.zeros((N, 128, 4 * T), np.float32)
    for r in range(N):
        e = entries(ids[r])
        for b in range(NB):
            X = mx_ref.quantize(np.ascontiguousarray(cut(x[r], b)))
            for k in range(4):
                c = 128 * (k * NB + b)
                y[r][:, c:c + 128] = mx_ref.matmul(U[e[4 * b + k]], X)
    return {"y": y}

@@ -1,0 +1,261 @@
+from concourse.bass import DstId, RemoteDMATransfer
+from concourse.mybir import dt, AluOpType, ActivationFunctionType
+
+NR, TILES, NBLK, CH = 4, 4, 8, 4
+CW = 32
+PART = TILES * CW
+COPY, IDENT = ActivationFunctionType.Copy, ActivationFunctionType.Identity
+UNIT = 2
+PIECES = {0: (4, 4), 1: (4, 4), 2: (4, 4), 3: (2, 2, 2, 2)}
+XLATE = 3
+
+SCRATCH = {
+    "wn": ("sbuf", [128, 2048], "bfloat16"),
+    "xb": ("sbuf", [128, 4096], "bfloat16"),
+    "xq": ("sbuf", [128, 1024], "float8_e4m3fn_x4"),
+    "xs": ("sbuf", [128, 1024], "uint8"),
+    "idr": ("sbuf", [128, 32], "int32"),
+    "idb": ("sbuf", [128, 32], "int32"),
+    "idf": ("sbuf", [128, 32], "float32"),
+    "ka": ("sbuf", [128, 32], "int32"),
+    "kb": ("sbuf", [128, 32], "int32"),
+    "km": ("sbuf", [128, 32], "float32"),
+    "pa": ("sbuf", [128, 8], "int32"),
+    "pb": ("sbuf", [128, 8], "int32"),
+    "ia": ("sbuf", [128, 8], "int32"),
+    "pu": ("sbuf", [128, 8], "float32"),
+    "ea": ("sbuf", [128, 32], "float32"),
+    "eb": ("sbuf", [128, 28], "float32"),
+    "sel": ("sbuf", [128, 8], "float32"),
+    "offf": ("sbuf", [128, 64], "float32"),
+    "off": ("sbuf", [128, 64], "uint16"),
+    "ps": ("psum", [128, 4096], "float32"),
+}
+for _c in range(CH):
+    SCRATCH["cw%d" % _c] = ("sbuf", [128, NR * PART], "float8_e4m3fn_x4")
+    SCRATCH["cs%d" % _c] = ("sbuf", [128, NR * PART], "uint8")
+    SCRATCH["w%d" % _c] = ("sbuf", [128, 512], "bfloat16")
+    SCRATCH["pk%d" % _c] = ("sbuf", [128, 1024], "float8_e4m3fn_x4")
+    SCRATCH["pp%d" % _c] = ("sbuf", [128, 1024], "uint8")
+    SCRATCH["yo%d" % _c] = ("sbuf", [128, 1024], "float32")
+
+SEMAPHORES = ["idl", "wl0", "wl1", "xl0", "xl1", "ga", "va", "sa", "ta", "loc", "out"] \
+    + ["hc%d" % c for c in range(CH)] + ["hs%d" % c for c in range(CH)] \
+    + ["ac%d" % c for c in range(CH)] + ["as%d" % c for c in range(CH)]
+
+
+def bits(es):
+    return sum(1 << e for e in es)
+
+
+def part(T, kind, c, r):
+    v = T["%s%d" % (kind, c)][:, PART * r:PART * r + PART]
+    return v.bitcast(dt.uint8) if kind == "cw" else v
+
+
+def send(T, topo, kind, c, r, dsts, es, sem):
+    ids = []
+    for q in dsts:
+        rid, pid, _s = topo.addr(q)
+        ids.append(DstId(rid=rid, pnc=pid))
+    return RemoteDMATransfer(dst_ids=ids, dma_engine_mask=bits(es), remote_sem=T.sem["%s%d" % (sem, c)],
+                             srcs=[part(T, kind, c, r)], dsts=[part(T, kind, c, r) for q in dsts])
+
+
+def others(T, r):
+    return [T.cores[(r + i) % NR] for i in range(1, NR)]
+
+
+def relays(T, topo, r):
+    me = T.cores[r]
+    ok = [c for c in topo.cores_of(me) if c != me and all(topo.may_write(c, d) for d in others(T, r))]
+    near = [c for c in ok if topo.die(c) == topo.die(me)]
+    far = [c for c in ok if topo.die(c) != topo.die(me)]
+    return far[:2] + near[:1]
+
+
+def on_chip(T, topo, r):
+    me = T.cores[r]
+    off = topo.engines(me, others(T, r)[0])
+    sp = [e for e in topo.engines(me, relays(T, topo, r)[0]) if e not in off]
+    h, q = len(sp) // 2, 3 * len(sp) // 4
+    return [[("cw", 2, 0, sp[:h]), ("cw", 3, 1, sp[h:])],
+            [("cs", 1, 2, sp[:h]), ("cs", 2, 2, sp[h:q]), ("cs", 3, 1, sp[q:])]]
+
+
+def relay_program(g, core, T, topo, r, i):
+    dsts = others(T, r)
+    es = topo.engines(core, dsts[0])
+    n = 0
+    for call in on_chip(T, topo, r):
+        for kind, c, j, got in call:
+            if j == i:
+                g.wait_ge(T.sem["h%s%d" % (kind[1].replace("w", "c"), c)], len(got))
+                g.remote_dma_fused([send(T, topo, kind, c, r, dsts, es, "ac" if kind == "cw" else "as")], local_sem=T.sem.loc)
+                n += len(es)
+    g.wait_ge(T.sem.loc, n)
+
+
+def rank_program(g, core, T, topo):
+    r = T.rank_of(core)
+    if r is None:
+        for q in range(NR):
+            hs = relays(T, topo, q)
+            if core in hs:
+                relay_program(g, core, T, topo, q, hs.index(core))
+        return
+    S = T.sem
+    V, A, P, Y = g.vector, g.scalar, g.tensor, g.sync
+    nv, na = [0], [0]
+
+    def v(ins):
+        ins.then_inc(S.va, 1)
+        nv[0] += 1
+        return nv[0]
+
+    def a(ins):
+        ins.then_inc(S.sa, 1)
+        na[0] += 1
+        return na[0]
+
+    for m in range(TILES):
+        (Y if m < 2 else A).dma_start(T.w0[:, 128 * m:128 * m + 128], T.wt[:, 512 * m:512 * m + 128]).then_inc(S.wl0, 16)
+    for m in range(TILES):
+        (Y if m < 2 else A).dma_start(T.wn[:, 512 * m + 128:512 * m + 512], T.wt[:, 512 * m + 128:512 * m + 512]).then_inc(S.wl1, 16)
+    Y.dma_start(T.idr[0:1, 0:32], T.ids[:, :]).then_inc(S.idl, 16)
+    A.dma_start(T.xb[:, 2048:4096], T.x[:, 2048:4096]).then_inc(S.xl1, 16)
+    Y.dma_start(T.xb[:, 0:2048], T.x[:, 0:2048]).then_inc(S.xl0, 16)
+
+    dsts = others(T, r)
+    hs = relays(T, topo, r)
+    far = topo.engines(core, dsts[0])
+    g.iota(T.ka[:, :], [[0, 4], [1, 4], [0, 2]], 0, 3).then_inc(S.ga, 1)
+    g.iota(T.pa[:, :], [[0, 8]], 0, 1).then_inc(S.ga, 1)
+    g.iota(T.ia[:, :], [[4, 8]], 0, 0).then_inc(S.ga, 1)
+
+    V.wait_ge(S.ga, 3)
+    v(V.tensor_scalar(T.kb[:, :], T.ka[:, :], 3, None, AluOpType.bitwise_and))
+    n = v(V.tensor_scalar(T.pb[:, :], T.pa[:, :], 2, 3, AluOpType.logical_shift_right, AluOpType.bitwise_and))
+    V.wait_ge(S.va, n)
+    v(V.tensor_scalar(T.km[:, :], T.kb[:, :], 0, CW, AluOpType.is_equal, AluOpType.mult))
+    v(V.tensor_tensor(T.pu[:, :], T.pb[:, :], T.ia[:, :], AluOpType.add))
+
+    quant = {}
+    cols = slice(PART * r, PART * r + PART)
+
+    def quantise(c):
+        quant[c] = v(V.quantize_mx(T["cw%d" % c][:, cols], T["cs%d" % c][:, cols], T["w%d" % c][:, :]))
+
+    V.wait_ge(S.wl0, 16 * TILES)
+    quantise(0)
+    A.wait_ge(S.wl1, 16 * TILES)
+    for m in range(TILES):
+        moved = a(A.activation(T.w3[:, 128 * m:128 * m + 128], T.wn[:, 512 * m + 384:512 * m + 512], COPY))
+    V.wait_ge(S.wl1, 16 * TILES)
+    for c in (2, 3, 1):
+        if c != 3:
+            for m in range(TILES):
+                n = v(V.tensor_copy(T["w%d" % c][:, 128 * m:128 * m + 128], T.wn[:, 512 * m + 128 * c:512 * m + 128 * c + 128]))
+            V.wait_ge(S.va, n)
+        else:
+            V.wait_ge(S.sa, moved)
+        quantise(c)
+
+    g.wait_ge(S.va, quant[0])
+    g.remote_dma_fused([send(T, topo, "cw", 0, r, dsts, far, "ac")], local_sem=S.loc)
+    g.remote_dma_fused([send(T, topo, "cs", 0, r, dsts, far, "as")], local_sem=S.loc)
+    left = 3 * len(far)
+    for call, c in zip(on_chip(T, topo, r), (3, 1)):
+        g.wait_ge(S.va, quant[c])
+        g.remote_dma_fused([send(T, topo, kind, k, r, [hs[j]], es, "hc" if kind == "cw" else "hs") for kind, k, j, es in call], local_sem=S.loc)
+        left += sum(len(es) for _k, _c, _j, es in call)
+    g.remote_dma_fused([send(T, topo, "cw", 1, r, dsts, far, "ac")], local_sem=S.loc)
+    g.wait_ge(S.idl, 16)
+    g.partition_broadcast(T.idb[:, :], T.idr[0:1, :], 128).then_inc(S.ga, 1)
+    g.wait_ge(S.loc, left)
+
+    V.wait_ge(S.ga, 4)
+    n = v(V.tensor_copy(T.idf[:, :], T.idb[:, :]))
+    V.wait_ge(S.va, n)
+    n = v(V.tensor_tensor(T.ea[:, :], T.idf[:, :], T.km[:, :], AluOpType.mult))
+    V.wait_ge(S.va, n)
+    n = v(V.tensor_tensor(T.eb[:, :], T.ea[:, 0:28], T.ea[:, 4:32], AluOpType.add))
+    V.wait_ge(S.va, n)
+    for q in range(2):
+        n = v(V.tensor_tensor(T.sel[:, 4 * q:4 * q + 4], T.eb[:, q:q + 25:8], T.eb[:, q + 2:q + 27:8], AluOpType.add))
+    A.wait_ge(S.va, n)
+    for ii in range(8):
+        m = a(A.activation(T.offf[:, ii:64:8], T.sel[:, :], IDENT, bias=T.pu[:, ii:ii + 1]))
+    xdone = {}
+
+    def quantise_x(q):
+        V.wait_ge(S["xl%d" % q], 16)
+        cs = slice(512 * q, 512 * q + 512)
+        xdone[q] = v(V.quantize_mx(T.xq[:, cs], T.xs[:, cs], T.xb[:, 2048 * q:2048 * q + 2048]))
+
+    quantise_x(0)
+    V.wait_ge(S.sa, m)
+    listed = v(V.tensor_copy(T.off[:, :], T.offf[:, :]))
+
+    nin = (NR - 1) * len(far)
+    pickv, picka, copyv, copya = {}, {}, {}, {}
+
+    def copies(c, b0):
+        for b in range(b0, b0 + UNIT):
+            o, i = T["yo%d" % c][:, 128 * b:128 * b + 128], T.ps[:, 512 * b:512 * b + 128]
+            if b % 2 == 0:
+                V.wait_ge(S.ta, NBLK * c + b + 1)
+                copyv[c, b] = v(V.tensor_copy(o, i))
+            else:
+                A.wait_ge(S.ta, NBLK * c + b + 1)
+                copya[c, b] = a(A.activation(o, i, COPY))
+
+    V.wait_ge(S.va, listed)
+    A.wait_ge(S.va, listed)
+    due, picks = [], 0
+    for c in range(CH):
+        V.wait_ge(S["ac%d" % c], nin)
+        A.wait_ge(S["as%d" % c], nin)
+        for b0 in range(0, NBLK, UNIT):
+            o, to = T.off[:, 8 * b0:8 * b0 + 8 * UNIT], slice(128 * b0, 128 * b0 + 128 * UNIT)
+            pickv[c, b0] = v(V.tensor_copy(T["pk%d" % c][:, to].bitcast(dt.uint32), T["cw%d" % c][:, 0:NR * PART].bitcast(dt.uint32).indirect(o)))
+            picka[c, b0] = a(A.activation(T["pp%d" % c][:, to], T["cs%d" % c][:, 0:NR * PART].indirect(o), COPY))
+            picks += 1
+            if picks == XLATE:
+                quantise_x(1)
+            for d in due:
+                copies(*d)
+            due = [(c, b0)]
+    for d in due:
+        copies(*d)
+
+    for c in range(CH):
+        for b0 in range(0, NBLK, UNIT):
+            P.wait_ge(S.va, max(pickv[c, b0], xdone[2 * b0 // NBLK]))
+            P.wait_ge(S.sa, picka[c, b0])
+            for b in range(b0, b0 + UNIT):
+                if c:
+                    if b % 2 == 0:
+                        P.wait_ge(S.va, copyv[c - 1, b])
+                    else:
+                        P.wait_ge(S.sa, copya[c - 1, b])
+                cs = slice(128 * b, 128 * b + 128)
+                P.matmul_mx(T.ps[:, 512 * b:512 * b + 128], T["pk%d" % c][:, cs], T["pp%d" % c][:, cs],
+                            T.xq[:, cs], T.xs[:, cs], True, True).then_inc(S.ta, 1)
+
+    nout = 0
+    for c in range(CH):
+        b0 = 0
+        for nb in PIECES[c]:
+            last = c == CH - 1 and b0 + nb == NBLK
+            for q in (Y, A) if last else (Y,):
+                q.wait_ge(S.va, copyv[c, b0 + nb - 2])
+                q.wait_ge(S.sa, copya[c, b0 + nb - 1])
+            for k in range(4):
+                (A if last and k % 2 else Y).dma_start(
+                    T.y[32 * c:32 * c + 32, 1024 * k + 128 * b0:1024 * k + 128 * (b0 + nb)],
+                    T["yo%d" % c][k:128:4, 128 * b0:128 * (b0 + nb)]).then_inc(S.out, 16)
+                nout += 1
+            b0 += nb
+    Y.wait_ge(S.ta, NBLK * CH)
+    Y.wait_ge(S.out, 16 * nout)

@@ -4,10 +4,14 @@ from concourse.mybir import dt, AluOpType, ActivationFunctionType
 NR, TILES, NBLK, CH = 4, 4, 8, 4
 CW = 32
 PART = TILES * CW
-COPY, IDENT = ActivationFunctionType.Copy, ActivationFunctionType.Identity
-UNIT = 2
-PIECES = {0: (4, 4), 1: (4, 4), 2: (4, 4), 3: (2, 2, 2, 2)}
-XLATE = 3
+COPY = ActivationFunctionType.Copy
+UNITS = {"0a": (0, 0, 2), "0b": (0, 2, 2), "0c": (0, 4, 4), "1a": (1, 0, 4), "1b": (1, 4, 4), "2a": (2, 0, 4), "2b": (2, 4, 4),
+         "3a": (3, 0, 4), "3b": (3, 4, 2), "3c": (3, 6, 2)}
+STORES = [(0, 0, 4), (0, 4, 4), (1, 0, 4), (1, 4, 4), (2, 0, 4), (2, 4, 4), (3, 0, 4), (3, 4, 2), (3, 6, 2)]
+STEPS = ["Q0", "Q1", "P0a", "P0b", "P0c", "C0a", "P1a", "C0b", "P1b", "C0c", "C1a", "P2a", "C1b", "P2b", "C2a",
+         "P3a", "C2b", "P3b", "C3a", "P3c", "C3b", "C3c"]
+SWAPPED = [(0, 1), (0, 3), (1, 1), (2, 1), (3, 1)]
+BANKS = 8
 
 SCRATCH = {
     "wn": ("sbuf", [128, 2048], "bfloat16"),
@@ -16,18 +20,10 @@ SCRATCH = {
     "xs": ("sbuf", [128, 1024], "uint8"),
     "idr": ("sbuf", [128, 32], "int32"),
     "idb": ("sbuf", [128, 32], "int32"),
-    "idf": ("sbuf", [128, 32], "float32"),
-    "ka": ("sbuf", [128, 32], "int32"),
-    "kb": ("sbuf", [128, 32], "int32"),
-    "km": ("sbuf", [128, 32], "float32"),
-    "pa": ("sbuf", [128, 8], "int32"),
-    "pb": ("sbuf", [128, 8], "int32"),
-    "ia": ("sbuf", [128, 8], "int32"),
-    "pu": ("sbuf", [128, 8], "float32"),
-    "ea": ("sbuf", [128, 32], "float32"),
-    "eb": ("sbuf", [128, 28], "float32"),
-    "sel": ("sbuf", [128, 8], "float32"),
-    "offf": ("sbuf", [128, 64], "float32"),
+    "pa": ("sbuf", [128, 2], "int32"),
+    "pb": ("sbuf", [128, 2], "int32"),
+    "ia": ("sbuf", [128, 2], "int32"),
+    "pu": ("sbuf", [128, 2], "float32"),
     "off": ("sbuf", [128, 64], "uint16"),
     "ps": ("psum", [128, 4096], "float32"),
 }
@@ -39,8 +35,7 @@ for _c in range(CH):
     SCRATCH["pp%d" % _c] = ("sbuf", [128, 1024], "uint8")
     SCRATCH["yo%d" % _c] = ("sbuf", [128, 1024], "float32")
 
-SEMAPHORES = ["idl", "wl0", "wl1", "xl0", "xl1", "ga", "va", "sa", "ta", "loc", "out"] \
-    + ["hc%d" % c for c in range(CH)] + ["hs%d" % c for c in range(CH)] \
+SEMAPHORES = ["idl", "wl", "xl0", "xl1", "ga", "va", "sa", "ta", "wl0", "loc", "out"] \
     + ["ac%d" % c for c in range(CH)] + ["as%d" % c for c in range(CH)]
 
 
@@ -74,25 +69,44 @@ def relays(T, topo, r):
     return far[:2] + near[:1]
 
 
-def on_chip(T, topo, r):
+def plan(T, topo, r):
     me = T.cores[r]
-    off = topo.engines(me, others(T, r)[0])
-    sp = [e for e in topo.engines(me, relays(T, topo, r)[0]) if e not in off]
-    h, q = len(sp) // 2, 3 * len(sp) // 4
-    return [[("cw", 2, 0, sp[:h]), ("cw", 3, 1, sp[h:])],
-            [("cs", 1, 2, sp[:h]), ("cs", 2, 2, sp[h:q]), ("cs", 3, 1, sp[q:])]]
+    every = others(T, r)
+    same = [d for d in every if topo.same_plane(topo.chip(me), topo.chip(d))]
+    cross = [d for d in every if d not in same]
+    f0, f1, n0 = relays(T, topo, r)
+    off = topo.engines(me, every[0])
+    on = [e for e in topo.engines(me, f0) if e not in off]
+    h, q = len(on) // 2, 3 * len(on) // 4
+    return {
+        me: [[("cw", 0, every, off)],
+             [("cs", 0, every, off), ("cs", 1, [n0], on)],
+             [("cw", 1, same + cross[:1], off), ("cw", 1, [f0], on)],
+             [("cw", 2, same, off), ("cw", 2, [f1], on)],
+             [("cs", 2, [n0], on[:h]), ("cs", 3, [f1], on[h:])],
+             [("cw", 3, same, off), ("cw", 3, [f0], on)]],
+        f0: [[("cw", 1, cross[1:], off)], [("cw", 3, cross, off)]],
+        f1: [[("cw", 2, cross, off)], [("cs", 3, every, off)]],
+        n0: [[("cs", 1, every, off)], [("cs", 2, every, off)]],
+    }
 
 
-def relay_program(g, core, T, topo, r, i):
-    dsts = others(T, r)
-    es = topo.engines(core, dsts[0])
+def landing(T, topo, core, kind, c):
+    return sum(len(es) for r in range(NR) for calls in plan(T, topo, r).values() for call in calls
+               for k, cc, ds, es in call if (k, cc) == (kind, c) and core in ds)
+
+
+def issue(g, T, topo, r, call, left):
+    g.remote_dma_fused([send(T, topo, kind, c, r, ds, es, "ac" if kind == "cw" else "as") for kind, c, ds, es in call], local_sem=left)
+    return sum(len(es) for _k, _c, _d, es in call)
+
+
+def relay_program(g, core, T, topo, r):
     n = 0
-    for call in on_chip(T, topo, r):
-        for kind, c, j, got in call:
-            if j == i:
-                g.wait_ge(T.sem["h%s%d" % (kind[1].replace("w", "c"), c)], len(got))
-                g.remote_dma_fused([send(T, topo, kind, c, r, dsts, es, "ac" if kind == "cw" else "as")], local_sem=T.sem.loc)
-                n += len(es)
+    for call in plan(T, topo, r)[core]:
+        for kind, c, _d, _e in call:
+            g.wait_ge(T.sem[("ac%d" if kind == "cw" else "as%d") % c], landing(T, topo, core, kind, c))
+        n += issue(g, T, topo, r, call, T.sem.loc)
     g.wait_ge(T.sem.loc, n)
 
 
@@ -100,9 +114,8 @@ def rank_program(g, core, T, topo):
     r = T.rank_of(core)
     if r is None:
         for q in range(NR):
-            hs = relays(T, topo, q)
-            if core in hs:
-                relay_program(g, core, T, topo, q, hs.index(core))
+            if core in plan(T, topo, q):
+                relay_program(g, core, T, topo, q)
         return
     S = T.sem
     V, A, P, Y = g.vector, g.scalar, g.tensor, g.sync
@@ -120,142 +133,145 @@ def rank_program(g, core, T, topo):
 
     for m in range(TILES):
         (Y if m < 2 else A).dma_start(T.w0[:, 128 * m:128 * m + 128], T.wt[:, 512 * m:512 * m + 128]).then_inc(S.wl0, 16)
-    for m in range(TILES):
-        (Y if m < 2 else A).dma_start(T.wn[:, 512 * m + 128:512 * m + 512], T.wt[:, 512 * m + 128:512 * m + 512]).then_inc(S.wl1, 16)
-    Y.dma_start(T.idr[0:1, 0:32], T.ids[:, :]).then_inc(S.idl, 16)
-    A.dma_start(T.xb[:, 2048:4096], T.x[:, 2048:4096]).then_inc(S.xl1, 16)
-    Y.dma_start(T.xb[:, 0:2048], T.x[:, 0:2048]).then_inc(S.xl0, 16)
+    Y.dma_start(T.wn[:, 128:2048], T.wt[:, 128:2048]).then_inc(S.wl, 16)
+    A.dma_start(T.idr[0:1, 0:32], T.ids[:, :]).then_inc(S.idl, 16)
+    A.dma_start(T.xb[:, 0:2048], T.x[:, 0:2048]).then_inc(S.xl0, 16)
+    Y.dma_start(T.xb[:, 2048:4096], T.x[:, 2048:4096]).then_inc(S.xl1, 16)
 
-    dsts = others(T, r)
-    hs = relays(T, topo, r)
-    far = topo.engines(core, dsts[0])
-    g.iota(T.ka[:, :], [[0, 4], [1, 4], [0, 2]], 0, 3).then_inc(S.ga, 1)
-    g.iota(T.pa[:, :], [[0, 8]], 0, 1).then_inc(S.ga, 1)
-    g.iota(T.ia[:, :], [[4, 8]], 0, 0).then_inc(S.ga, 1)
+    g.iota(T.pa[:, :], [[0, 2]], 0, 1).then_inc(S.ga, 1)
+    g.iota(T.ia[:, :], [[16, 2]], 0, 0).then_inc(S.ga, 1)
 
-    V.wait_ge(S.ga, 3)
-    v(V.tensor_scalar(T.kb[:, :], T.ka[:, :], 3, None, AluOpType.bitwise_and))
-    n = v(V.tensor_scalar(T.pb[:, :], T.pa[:, :], 2, 3, AluOpType.logical_shift_right, AluOpType.bitwise_and))
+    V.wait_ge(S.ga, 2)
+    n = v(V.tensor_scalar(T.pb[:, :], T.pa[:, :], 15, None, AluOpType.bitwise_and))
     V.wait_ge(S.va, n)
-    v(V.tensor_scalar(T.km[:, :], T.kb[:, :], 0, CW, AluOpType.is_equal, AluOpType.mult))
-    v(V.tensor_tensor(T.pu[:, :], T.pb[:, :], T.ia[:, :], AluOpType.add))
+    const = v(V.tensor_tensor(T.pu[:, :], T.pb[:, :], T.ia[:, :], AluOpType.add))
 
-    quant = {}
+    quant, moved = {}, {}
     cols = slice(PART * r, PART * r + PART)
 
-    def quantise(c):
+    def piece(c, m):
+        return T["w%d" % c][:, 128 * m:128 * m + 128], T.wn[:, 512 * m + 128 * c:512 * m + 128 * c + 128]
+
+    by_a = [(1, 0), (2, 0), (2, 1), (3, 0), (3, 1)]
+    A.wait_ge(S.wl, 16)
+    for c, m in by_a:
+        moved[c] = a(A.activation(*piece(c, m), COPY))
+    V.wait_ge(S.wl0, 16 * TILES)
+    for c in range(CH):
+        n = 0
+        if c == 1:
+            V.wait_ge(S.wl, 16)
+        for m in range(TILES):
+            if c and (c, m) not in by_a:
+                n = v(V.tensor_copy(*piece(c, m)))
+        if n:
+            V.wait_ge(S.va, n)
+        if c in moved:
+            V.wait_ge(S.sa, moved[c])
         quant[c] = v(V.quantize_mx(T["cw%d" % c][:, cols], T["cs%d" % c][:, cols], T["w%d" % c][:, :]))
 
-    V.wait_ge(S.wl0, 16 * TILES)
-    quantise(0)
-    A.wait_ge(S.wl1, 16 * TILES)
-    for m in range(TILES):
-        moved = a(A.activation(T.w3[:, 128 * m:128 * m + 128], T.wn[:, 512 * m + 384:512 * m + 512], COPY))
-    V.wait_ge(S.wl1, 16 * TILES)
-    for c in (2, 3, 1):
-        if c != 3:
-            for m in range(TILES):
-                n = v(V.tensor_copy(T["w%d" % c][:, 128 * m:128 * m + 128], T.wn[:, 512 * m + 128 * c:512 * m + 128 * c + 128]))
-            V.wait_ge(S.va, n)
-        else:
-            V.wait_ge(S.sa, moved)
-        quantise(c)
-
-    g.wait_ge(S.va, quant[0])
-    g.remote_dma_fused([send(T, topo, "cw", 0, r, dsts, far, "ac")], local_sem=S.loc)
-    g.remote_dma_fused([send(T, topo, "cs", 0, r, dsts, far, "as")], local_sem=S.loc)
-    left = 3 * len(far)
-    for call, c in zip(on_chip(T, topo, r), (3, 1)):
-        g.wait_ge(S.va, quant[c])
-        g.remote_dma_fused([send(T, topo, kind, k, r, [hs[j]], es, "hc" if kind == "cw" else "hs") for kind, k, j, es in call], local_sem=S.loc)
-        left += sum(len(es) for _k, _c, _j, es in call)
-    g.remote_dma_fused([send(T, topo, "cw", 1, r, dsts, far, "ac")], local_sem=S.loc)
-    g.wait_ge(S.idl, 16)
-    g.partition_broadcast(T.idb[:, :], T.idr[0:1, :], 128).then_inc(S.ga, 1)
+    left, seen = 0, 0
+    for call in plan(T, topo, r)[core]:
+        need = max(quant[c] for _k, c, _d, _e in call)
+        if need > seen:
+            g.wait_ge(S.va, need)
+            seen = need
+        first = not left
+        left += issue(g, T, topo, r, call, S.loc)
+        if first:
+            g.wait_ge(S.idl, 16)
+            g.partition_broadcast(T.idb[:, :], T.idr[0:1, :], 128).then_inc(S.ga, 1)
     g.wait_ge(S.loc, left)
 
-    V.wait_ge(S.ga, 4)
-    n = v(V.tensor_copy(T.idf[:, :], T.idb[:, :]))
-    V.wait_ge(S.va, n)
-    n = v(V.tensor_tensor(T.ea[:, :], T.idf[:, :], T.km[:, :], AluOpType.mult))
-    V.wait_ge(S.va, n)
-    n = v(V.tensor_tensor(T.eb[:, :], T.ea[:, 0:28], T.ea[:, 4:32], AluOpType.add))
-    V.wait_ge(S.va, n)
-    for q in range(2):
-        n = v(V.tensor_tensor(T.sel[:, 4 * q:4 * q + 4], T.eb[:, q:q + 25:8], T.eb[:, q + 2:q + 27:8], AluOpType.add))
-    A.wait_ge(S.va, n)
-    for ii in range(8):
-        m = a(A.activation(T.offf[:, ii:64:8], T.sel[:, :], IDENT, bias=T.pu[:, ii:ii + 1]))
-    xdone = {}
+    V.wait_ge(S.ga, 3)
+    for s in range(2):
+        for h in range(2):
+            listed = v(V.tensor_scalar(T.off[:, 32 * s + h:32 * s + 32:2], T.idb[:, s:32:2], CW, T.pu[:, h:h + 1],
+                                       AluOpType.mult, AluOpType.add))
+    xdone, picked, copied = {}, {}, {}
+    order = [UNITS[s[1:]] for s in STEPS if s[0] == "C"]
+
+    def groups(c, b0, nb):
+        n = 1
+        return [(b, n) for b in range(b0, b0 + nb, n)]
+
+    allgroups = [(c, b, n) for c, b0, nb in order for b, n in groups(c, b0, nb)]
+    product, issued = {}, {}
+    for c, b0, nb in order:
+        for b, n in groups(c, b0, nb):
+            if n == 2:
+                product[c, b + 1] = len(product) + 1
+        for b, n in groups(c, b0, nb):
+            product[c, b] = len(product) + 1
+
+    def bank(c, b, n):
+        return 512 * (allgroups.index((c, b, n)) % BANKS)
 
     def quantise_x(q):
         V.wait_ge(S["xl%d" % q], 16)
         cs = slice(512 * q, 512 * q + 512)
         xdone[q] = v(V.quantize_mx(T.xq[:, cs], T.xs[:, cs], T.xb[:, 2048 * q:2048 * q + 2048]))
 
-    quantise_x(0)
-    V.wait_ge(S.sa, m)
-    listed = v(V.tensor_copy(T.off[:, :], T.offf[:, :]))
+    def picks(c, b0, nb):
+        if (c, 0) not in picked:
+            V.wait_ge(S["ac%d" % c], landing(T, topo, core, "cw", c))
+            A.wait_ge(S["as%d" % c], landing(T, topo, core, "cs", c))
+        o, to = T.off[:, 8 * b0:8 * (b0 + nb)], slice(128 * b0, 128 * (b0 + nb))
+        picked[c, b0] = (
+            v(V.tensor_copy(T["pk%d" % c][:, to].bitcast(dt.uint32), T["cw%d" % c][:, 0:NR * PART].bitcast(dt.uint32).indirect(o))),
+            a(A.activation(T["pp%d" % c][:, to], T["cs%d" % c][:, 0:NR * PART].indirect(o), COPY)))
 
-    nin = (NR - 1) * len(far)
-    pickv, picka, copyv, copya = {}, {}, {}, {}
-
-    def copies(c, b0):
-        for b in range(b0, b0 + UNIT):
-            o, i = T["yo%d" % c][:, 128 * b:128 * b + 128], T.ps[:, 512 * b:512 * b + 128]
-            if b % 2 == 0:
-                V.wait_ge(S.ta, NBLK * c + b + 1)
-                copyv[c, b] = v(V.tensor_copy(o, i))
+    def copies(c, b0, nb):
+        for b, n in groups(c, b0, nb):
+            o, i = T["yo%d" % c][:, 128 * b:128 * (b + n)], T.ps[:, bank(c, b, n):bank(c, b, n) + 128 * n]
+            if (allgroups.index((c, b, n)) % 2 == 0) != ((c, b) in SWAPPED):
+                V.wait_ge(S.ta, product[c, b])
+                copied[c, b] = ("va", v(V.tensor_copy(o, i)))
             else:
-                A.wait_ge(S.ta, NBLK * c + b + 1)
-                copya[c, b] = a(A.activation(o, i, COPY))
+                A.wait_ge(S.ta, product[c, b])
+                copied[c, b] = ("sa", a(A.activation(o, i, COPY)))
 
     V.wait_ge(S.va, listed)
     A.wait_ge(S.va, listed)
-    due, picks = [], 0
-    for c in range(CH):
-        V.wait_ge(S["ac%d" % c], nin)
-        A.wait_ge(S["as%d" % c], nin)
-        for b0 in range(0, NBLK, UNIT):
-            o, to = T.off[:, 8 * b0:8 * b0 + 8 * UNIT], slice(128 * b0, 128 * b0 + 128 * UNIT)
-            pickv[c, b0] = v(V.tensor_copy(T["pk%d" % c][:, to].bitcast(dt.uint32), T["cw%d" % c][:, 0:NR * PART].bitcast(dt.uint32).indirect(o)))
-            picka[c, b0] = a(A.activation(T["pp%d" % c][:, to], T["cs%d" % c][:, 0:NR * PART].indirect(o), COPY))
-            picks += 1
-            if picks == XLATE:
-                quantise_x(1)
-            for d in due:
-                copies(*d)
-            due = [(c, b0)]
-    for d in due:
-        copies(*d)
+    for s in STEPS:
+        if s[0] == "Q":
+            quantise_x(int(s[1]))
+        else:
+            (picks if s[0] == "P" else copies)(*UNITS[s[1:]])
 
-    for c in range(CH):
-        for b0 in range(0, NBLK, UNIT):
-            P.wait_ge(S.va, max(pickv[c, b0], xdone[2 * b0 // NBLK]))
-            P.wait_ge(S.sa, picka[c, b0])
-            for b in range(b0, b0 + UNIT):
-                if c:
-                    if b % 2 == 0:
-                        P.wait_ge(S.va, copyv[c - 1, b])
-                    else:
-                        P.wait_ge(S.sa, copya[c - 1, b])
-                cs = slice(128 * b, 128 * b + 128)
-                P.matmul_mx(T.ps[:, 512 * b:512 * b + 128], T["pk%d" % c][:, cs], T["pp%d" % c][:, cs],
+    for c, b0, nb in order:
+        P.wait_ge(S.va, max(picked[c, b0][0], xdone[2 * b0 // NBLK]))
+        P.wait_ge(S.sa, picked[c, b0][1])
+        todo = groups(c, b0, nb)
+        for wide in (True, False):
+            for b, n in todo:
+                if wide and n == 1:
+                    continue
+                i = allgroups.index((c, b, n))
+                if (wide or n == 1) and i >= BANKS:
+                    sem, cnt = copied[allgroups[i - BANKS][:2]]
+                    P.wait_ge(S[sem], cnt)
+                if not wide and n == 2:
+                    P.wait_ge(S.ta, issued[c, b + 1])
+                w = b + 1 if wide else b
+                ws, cs = slice(128 * w, 128 * w + 128), slice(128 * b, 128 * w + 128)
+                P.matmul_mx(T.ps[:, bank(c, b, n):bank(c, b, n) + 128 * (w - b + 1)], T["pk%d" % c][:, ws], T["pp%d" % c][:, ws],
                             T.xq[:, cs], T.xs[:, cs], True, True).then_inc(S.ta, 1)
+                issued[c, w] = len(issued) + 1
+                assert issued[c, w] == product[c, w]
 
     nout = 0
-    for c in range(CH):
-        b0 = 0
-        for nb in PIECES[c]:
-            last = c == CH - 1 and b0 + nb == NBLK
-            for q in (Y, A) if last else (Y,):
-                q.wait_ge(S.va, copyv[c, b0 + nb - 2])
-                q.wait_ge(S.sa, copya[c, b0 + nb - 1])
-            for k in range(4):
-                (A if last and k % 2 else Y).dma_start(
-                    T.y[32 * c:32 * c + 32, 1024 * k + 128 * b0:1024 * k + 128 * (b0 + nb)],
-                    T["yo%d" % c][k:128:4, 128 * b0:128 * (b0 + nb)]).then_inc(S.out, 16)
-                nout += 1
-            b0 += nb
+    for c, b0, nb in STORES:
+        last = (c, b0, nb) == STORES[-1]
+        for q in (Y, A) if last else (Y,):
+            for sem in ("va", "sa"):
+                ns = [copied[c, b][1] for b, n in groups(c, b0, nb) if copied[c, b][0] == sem]
+                if ns:
+                    q.wait_ge(S[sem], max(ns))
+        for k in range(4):
+            (A if last and k % 2 else Y).dma_start(
+                T.y[32 * c:32 * c + 32, 1024 * k + 128 * b0:1024 * k + 128 * (b0 + nb)],
+                T["yo%d" % c][32 * k:32 * k + 32, 128 * b0:128 * (b0 + nb)]).then_inc(S.out, 16)
+            nout += 1
     Y.wait_ge(S.ta, NBLK * CH)
     Y.wait_ge(S.out, 16 * nout)

from concourse.bass import DstId, RemoteDMATransfer
from concourse.mybir import dt, AluOpType, ActivationFunctionType

NR, TILES, NBLK, CH = 4, 4, 8, 4
CW = 32
PART = TILES * CW
COPY = ActivationFunctionType.Copy
UNITS = {"0a": (0, 0, 2), "0b": (0, 2, 2), "0c": (0, 4, 4), "1a": (1, 0, 4), "1b": (1, 4, 4), "2a": (2, 0, 4), "2b": (2, 4, 4),
         "3a": (3, 0, 4), "3b": (3, 4, 2), "3c": (3, 6, 2)}
STORES = [(0, 0, 4), (0, 4, 4), (1, 0, 4), (1, 4, 4), (2, 0, 4), (2, 4, 4), (3, 0, 4), (3, 4, 2), (3, 6, 2)]
STEPS = ["Q0", "Q1", "P0a", "P0b", "P0c", "C0a", "P1a", "C0b", "P1b", "C0c", "C1a", "P2a", "C1b", "P2b", "C2a",
         "P3a", "C2b", "P3b", "C3a", "P3c", "C3b", "C3c"]
SWAPPED = [(0, 1), (0, 3), (1, 1), (2, 1), (3, 1)]
BANKS = 8

SCRATCH = {
    "wn": ("sbuf", [128, 2048], "bfloat16"),
    "xb": ("sbuf", [128, 4096], "bfloat16"),
    "xq": ("sbuf", [128, 1024], "float8_e4m3fn_x4"),
    "xs": ("sbuf", [128, 1024], "uint8"),
    "idr": ("sbuf", [128, 32], "int32"),
    "idb": ("sbuf", [128, 32], "int32"),
    "pa": ("sbuf", [128, 2], "int32"),
    "pb": ("sbuf", [128, 2], "int32"),
    "ia": ("sbuf", [128, 2], "int32"),
    "pu": ("sbuf", [128, 2], "float32"),
    "off": ("sbuf", [128, 64], "uint16"),
    "ps": ("psum", [128, 4096], "float32"),
}
for _c in range(CH):
    SCRATCH["cw%d" % _c] = ("sbuf", [128, NR * PART], "float8_e4m3fn_x4")
    SCRATCH["cs%d" % _c] = ("sbuf", [128, NR * PART], "uint8")
    SCRATCH["w%d" % _c] = ("sbuf", [128, 512], "bfloat16")
    SCRATCH["pk%d" % _c] = ("sbuf", [128, 1024], "float8_e4m3fn_x4")
    SCRATCH["pp%d" % _c] = ("sbuf", [128, 1024], "uint8")
    SCRATCH["yo%d" % _c] = ("sbuf", [128, 1024], "float32")

SEMAPHORES = ["idl", "wl", "xl0", "xl1", "ga", "va", "sa", "ta", "wl0", "loc", "out"] \
    + ["ac%d" % c for c in range(CH)] + ["as%d" % c for c in range(CH)]


def bits(es):
    return sum(1 << e for e in es)


def part(T, kind, c, r):
    v = T["%s%d" % (kind, c)][:, PART * r:PART * r + PART]
    return v.bitcast(dt.uint8) if kind == "cw" else v


def send(T, topo, kind, c, r, dsts, es, sem):
    ids = []
    for q in dsts:
        rid, pid, _s = topo.addr(q)
        ids.append(DstId(rid=rid, pnc=pid))
    return RemoteDMATransfer(dst_ids=ids, dma_engine_mask=bits(es), remote_sem=T.sem["%s%d" % (sem, c)],
                             srcs=[part(T, kind, c, r)], dsts=[part(T, kind, c, r) for q in dsts])


def others(T, r):
    return [T.cores[(r + i) % NR] for i in range(1, NR)]


def relays(T, topo, r):
    me = T.cores[r]
    ok = [c for c in topo.cores_of(me) if c != me and all(topo.may_write(c, d) for d in others(T, r))]
    near = [c for c in ok if topo.die(c) == topo.die(me)]
    far = [c for c in ok if topo.die(c) != topo.die(me)]
    return far[:2] + near[:1]


def plan(T, topo, r):
    me = T.cores[r]
    every = others(T, r)
    same = [d for d in every if topo.same_plane(topo.chip(me), topo.chip(d))]
    cross = [d for d in every if d not in same]
    f0, f1, n0 = relays(T, topo, r)
    off = topo.engines(me, every[0])
    on = [e for e in topo.engines(me, f0) if e not in off]
    h, q = len(on) // 2, 3 * len(on) // 4
    return {
        me: [[("cw", 0, every, off)],
             [("cs", 0, every, off), ("cs", 1, [n0], on)],
             [("cw", 1, same + cross[:1], off), ("cw", 1, [f0], on)],
             [("cw", 2, same, off), ("cw", 2, [f1], on)],
             [("cs", 2, [n0], on[:h]), ("cs", 3, [f1], on[h:])],
             [("cw", 3, same, off), ("cw", 3, [f0], on)]],
        f0: [[("cw", 1, cross[1:], off)], [("cw", 3, cross, off)]],
        f1: [[("cw", 2, cross, off)], [("cs", 3, every, off)]],
        n0: [[("cs", 1, every, off)], [("cs", 2, every, off)]],
    }


def landing(T, topo, core, kind, c):
    return sum(len(es) for r in range(NR) for calls in plan(T, topo, r).values() for call in calls
               for k, cc, ds, es in call if (k, cc) == (kind, c) and core in ds)


def issue(g, T, topo, r, call, left):
    g.remote_dma_fused([send(T, topo, kind, c, r, ds, es, "ac" if kind == "cw" else "as") for kind, c, ds, es in call], local_sem=left)
    return sum(len(es) for _k, _c, _d, es in call)


def relay_program(g, core, T, topo, r):
    n = 0
    for call in plan(T, topo, r)[core]:
        for kind, c, _d, _e in call:
            g.wait_ge(T.sem[("ac%d" if kind == "cw" else "as%d") % c], landing(T, topo, core, kind, c))
        n += issue(g, T, topo, r, call, T.sem.loc)
    g.wait_ge(T.sem.loc, n)


def rank_program(g, core, T, topo):
    r = T.rank_of(core)
    if r is None:
        for q in range(NR):
            if core in plan(T, topo, q):
                relay_program(g, core, T, topo, q)
        return
    S = T.sem
    V, A, P, Y = g.vector, g.scalar, g.tensor, g.sync
    nv, na = [0], [0]

    def v(ins):
        ins.then_inc(S.va, 1)
        nv[0] += 1
        return nv[0]

    def a(ins):
        ins.then_inc(S.sa, 1)
        na[0] += 1
        return na[0]

    for m in range(TILES):
        (Y if m < 2 else A).dma_start(T.w0[:, 128 * m:128 * m + 128], T.wt[:, 512 * m:512 * m + 128]).then_inc(S.wl0, 16)
    Y.dma_start(T.wn[:, 128:2048], T.wt[:, 128:2048]).then_inc(S.wl, 16)
    A.dma_start(T.idr[0:1, 0:32], T.ids[:, :]).then_inc(S.idl, 16)
    A.dma_start(T.xb[:, 0:2048], T.x[:, 0:2048]).then_inc(S.xl0, 16)
    Y.dma_start(T.xb[:, 2048:4096], T.x[:, 2048:4096]).then_inc(S.xl1, 16)

    g.iota(T.pa[:, :], [[0, 2]], 0, 1).then_inc(S.ga, 1)
    g.iota(T.ia[:, :], [[16, 2]], 0, 0).then_inc(S.ga, 1)

    V.wait_ge(S.ga, 2)
    n = v(V.tensor_scalar(T.pb[:, :], T.pa[:, :], 15, None, AluOpType.bitwise_and))
    V.wait_ge(S.va, n)
    const = v(V.tensor_tensor(T.pu[:, :], T.pb[:, :], T.ia[:, :], AluOpType.add))

    quant, moved = {}, {}
    cols = slice(PART * r, PART * r + PART)

    def piece(c, m):
        return T["w%d" % c][:, 128 * m:128 * m + 128], T.wn[:, 512 * m + 128 * c:512 * m + 128 * c + 128]

    by_a = [(1, 0), (2, 0), (2, 1), (3, 0), (3, 1)]
    A.wait_ge(S.wl, 16)
    for c, m in by_a:
        moved[c] = a(A.activation(*piece(c, m), COPY))
    V.wait_ge(S.wl0, 16 * TILES)
    for c in range(CH):
        n = 0
        if c == 1:
            V.wait_ge(S.wl, 16)
        for m in range(TILES):
            if c and (c, m) not in by_a:
                n = v(V.tensor_copy(*piece(c, m)))
        if n:
            V.wait_ge(S.va, n)
        if c in moved:
            V.wait_ge(S.sa, moved[c])
        quant[c] = v(V.quantize_mx(T["cw%d" % c][:, cols], T["cs%d" % c][:, cols], T["w%d" % c][:, :]))

    left, seen = 0, 0
    for call in plan(T, topo, r)[core]:
        need = max(quant[c] for _k, c, _d, _e in call)
        if need > seen:
            g.wait_ge(S.va, need)
            seen = need
        first = not left
        left += issue(g, T, topo, r, call, S.loc)
        if first:
            g.wait_ge(S.idl, 16)
            g.partition_broadcast(T.idb[:, :], T.idr[0:1, :], 128).then_inc(S.ga, 1)
    g.wait_ge(S.loc, left)

    V.wait_ge(S.ga, 3)
    for s in range(2):
        for h in range(2):
            listed = v(V.tensor_scalar(T.off[:, 32 * s + h:32 * s + 32:2], T.idb[:, s:32:2], CW, T.pu[:, h:h + 1],
                                       AluOpType.mult, AluOpType.add))
    xdone, picked, copied = {}, {}, {}
    order = [UNITS[s[1:]] for s in STEPS if s[0] == "C"]

    def groups(c, b0, nb):
        n = 1
        return [(b, n) for b in range(b0, b0 + nb, n)]

    allgroups = [(c, b, n) for c, b0, nb in order for b, n in groups(c, b0, nb)]
    product, issued = {}, {}
    for c, b0, nb in order:
        for b, n in groups(c, b0, nb):
            if n == 2:
                product[c, b + 1] = len(product) + 1
        for b, n in groups(c, b0, nb):
            product[c, b] = len(product) + 1

    def bank(c, b, n):
        return 512 * (allgroups.index((c, b, n)) % BANKS)

    def quantise_x(q):
        V.wait_ge(S["xl%d" % q], 16)
        cs = slice(512 * q, 512 * q + 512)
        xdone[q] = v(V.quantize_mx(T.xq[:, cs], T.xs[:, cs], T.xb[:, 2048 * q:2048 * q + 2048]))

    def picks(c, b0, nb):
        if (c, 0) not in picked:
            V.wait_ge(S["ac%d" % c], landing(T, topo, core, "cw", c))
            A.wait_ge(S["as%d" % c], landing(T, topo, core, "cs", c))
        o, to = T.off[:, 8 * b0:8 * (b0 + nb)], slice(128 * b0, 128 * (b0 + nb))
        picked[c, b0] = (
            v(V.tensor_copy(T["pk%d" % c][:, to].bitcast(dt.uint32), T["cw%d" % c][:, 0:NR * PART].bitcast(dt.uint32).indirect(o))),
            a(A.activation(T["pp%d" % c][:, to], T["cs%d" % c][:, 0:NR * PART].indirect(o), COPY)))

    def copies(c, b0, nb):
        for b, n in groups(c, b0, nb):
            o, i = T["yo%d" % c][:, 128 * b:128 * (b + n)], T.ps[:, bank(c, b, n):bank(c, b, n) + 128 * n]
            if (allgroups.index((c, b, n)) % 2 == 0) != ((c, b) in SWAPPED):
                V.wait_ge(S.ta, product[c, b])
                copied[c, b] = ("va", v(V.tensor_copy(o, i)))
            else:
                A.wait_ge(S.ta, product[c, b])
                copied[c, b] = ("sa", a(A.activation(o, i, COPY)))

    V.wait_ge(S.va, listed)
    A.wait_ge(S.va, listed)
    for s in STEPS:
        if s[0] == "Q":
            quantise_x(int(s[1]))
        else:
            (picks if s[0] == "P" else copies)(*UNITS[s[1:]])

    for c, b0, nb in order:
        P.wait_ge(S.va, max(picked[c, b0][0], xdone[2 * b0 // NBLK]))
        P.wait_ge(S.sa, picked[c, b0][1])
        todo = groups(c, b0, nb)
        for wide in (True, False):
            for b, n in todo:
                if wide and n == 1:
                    continue
                i = allgroups.index((c, b, n))
                if (wide or n == 1) and i >= BANKS:
                    sem, cnt = copied[allgroups[i - BANKS][:2]]
                    P.wait_ge(S[sem], cnt)
                if not wide and n == 2:
                    P.wait_ge(S.ta, issued[c, b + 1])
                w = b + 1 if wide else b
                ws, cs = slice(128 * w, 128 * w + 128), slice(128 * b, 128 * w + 128)
                P.matmul_mx(T.ps[:, bank(c, b, n):bank(c, b, n) + 128 * (w - b + 1)], T["pk%d" % c][:, ws], T["pp%d" % c][:, ws],
                            T.xq[:, cs], T.xs[:, cs], True, True).then_inc(S.ta, 1)
                issued[c, w] = len(issued) + 1
                assert issued[c, w] == product[c, w]

    nout = 0
    for c, b0, nb in STORES:
        last = (c, b0, nb) == STORES[-1]
        for q in (Y, A) if last else (Y,):
            for sem in ("va", "sa"):
                ns = [copied[c, b][1] for b, n in groups(c, b0, nb) if copied[c, b][0] == sem]
                if ns:
                    q.wait_ge(S[sem], max(ns))
        for k in range(4):
            (A if last and k % 2 else Y).dma_start(
                T.y[32 * c:32 * c + 32, 1024 * k + 128 * b0:1024 * k + 128 * (b0 + nb)],
                T["yo%d" % c][32 * k:32 * k + 32, 128 * b0:128 * (b0 + nb)]).then_inc(S.out, 16)
            nout += 1
    Y.wait_ge(S.ta, NBLK * CH)
    Y.wait_ge(S.out, 16 * nout)
